import numpy as np
import ml_dtypes


def mxq(x, axis, fmt="e4m3"):
    dtype, down = {"e4m3": (ml_dtypes.float8_e4m3fn, 7), "e5m2": (ml_dtypes.float8_e5m2, 14)}[fmt]
    v = np.moveaxis(np.asarray(x, np.float32).astype(ml_dtypes.bfloat16).astype(np.float64), axis, -1)
    blocks = v.reshape(v.shape[:-1] + (-1, 32))
    amax = np.abs(blocks).max(-1, keepdims=True)
    byte = np.maximum(np.where(amax > 0, np.frexp(amax)[1] - 1 + 127, 0) - down, 1)
    scale = np.exp2(byte - 127.0)
    codes = (blocks / scale).astype(np.float32).astype(dtype).astype(np.float64)
    return np.moveaxis((codes * scale).reshape(v.shape), -1, axis)


WIDE = False


def mx_kscale(k):
    if not WIDE:
        return np.ones(k)
    levels = np.array([10, -10, 5, -5, 0])
    if k % 512:
        return np.exp2(np.random.permutation(np.resize(levels, k // 32))).repeat(32)
    a = np.empty((k // 512, 16))
    for p in range(k // 512):
        a[p, :8] = np.random.permutation(np.resize(levels, 8))
        for g in range(8):
            far = levels[np.abs(levels - a[p, g]) >= 10]
            a[p, g + 8] = far[np.random.randint(len(far))]
    return np.exp2(a.ravel()).repeat(32)


def f64(x):
    return np.asarray(x).astype(np.float64)


def striped(idx):
    return np.tile(idx.reshape(-1, 16).T, (8, 1)).astype(np.uint16)


def unstriped(offs):
    return offs[:16].T.reshape(-1).astype(np.int64)


def striped8(idx):
    return np.concatenate([x.reshape(-1, 16).T for x in idx]).astype(np.uint16)


def runs(offs, k):
    lists = np.stack([offs[16 * r : 16 * r + 16].T.reshape(-1) for r in range(8)]).astype(np.int64)
    return lists[np.arange(k) % 512 // 64]


def pack_weight(w):
    k, n = w.shape
    w = f64(np.asarray(w, np.float32).astype(ml_dtypes.bfloat16)).reshape(k // 32, 32, n)
    amax = np.abs(w).max(1)
    byte = np.clip(np.where(amax > 0, np.frexp(amax)[1] - 1 + 127 - 7, 1), 1, 254)
    scaled = (w * np.exp2(127.0 - byte)[:, None, :]).reshape(k, n).astype(np.float32)
    words = np.ascontiguousarray(scaled.reshape(k // 512, 128, 4, n).transpose(0, 1, 3, 2)).astype(ml_dtypes.float8_e4m3fn).view(np.uint8)
    return words, np.ascontiguousarray(byte.astype(np.uint8).reshape(k // 512, 16, n))


def unpack_weight(words, scales):
    g, p, n, _ = words.shape
    vals = np.ascontiguousarray(words).view(ml_dtypes.float8_e4m3fn).astype(np.float64) * np.repeat(np.exp2(scales.astype(np.float64) - 127.0), 8, axis=1)[..., None]
    return vals.transpose(0, 1, 3, 2).reshape(g * 512, n)


K, T, S, N, G, H, U = 512, 2048, 256, 512, 2048, 512, 512


def setup_inputs():
    n = np.random.standard_normal
    s = mx_kscale(K)[:, None]
    u = mx_kscale(K)
    packed_xT = pack_weight(n((K, T)) * s)
    packed_dT = pack_weight(n((K, G)) / s)
    perm = np.random.permutation(U)
    return {
        "x_words": packed_xT[0],
        "x_scales": packed_xT[1],
        "d_words": packed_dT[0],
        "d_scales": packed_dT[1],
        "gn": (np.random.uniform(0.5, 1.5, (H, 1)) * u[:, None]).astype(np.float32),
        "w1": (n((H, N)) / np.sqrt(H) / u[:, None]).astype(np.float32),
        "offs": striped(np.random.permutation(T)[:S]),
        "ci": striped(np.random.permutation(G)[:H]),
        "n1": striped8(np.stack([np.random.permutation(S) for _ in range(8)])),
        "n2": striped8(np.stack([np.random.permutation(S) for _ in range(8)])),
        "n3": striped(perm[:S]),
        "n4": striped(perm[S:]),
        "n5": striped(np.random.permutation(S)),
    }


def reference(x_words, x_scales, d_words, d_scales, gn, w1, offs, ci, n1, n2, n3, n4, n5):
    d_ci = unpack_weight(d_words, d_scales)[:, unstriped(ci)]
    xq = unpack_weight(x_words, x_scales)[:, unstriped(offs)]
    s = 0.0625 * (d_ci.T @ xq)
    st = np.maximum(s, s[np.arange(H)[:, None], runs(n1, H)])
    z = f64(gn) * (st[np.arange(H)[:, None], runs(n2, H)] - (0.5 * s))
    h = mxq(f64(w1), 0, "e4m3").T @ mxq(z, 0, "e4m3")
    nw = h - h[:, unstriped(n5)]
    ph = np.zeros((N, U))
    ph[:, unstriped(n3)] = h
    out = ph.copy()
    out[:, unstriped(n4)] = nw
    return out

@@ -1,0 +1,146 @@
+from contextlib import ExitStack
+
+import concourse.mybir as mybir
+
+K, T, G, S, H, N, U = 512, 2048, 2048, 256, 512, 512, 512
+FLOPS = 2 * K * H * S + 2 * H * N * S
+
+F32 = mybir.dt.float32
+BF16 = mybir.dt.bfloat16
+I32 = mybir.dt.int32
+U32 = mybir.dt.uint32
+U16 = mybir.dt.uint16
+U8 = mybir.dt.uint8
+FP8X4 = mybir.dt.float8_e4m3fn_x4
+ALU = mybir.AluOpType
+COPY = mybir.ActivationFunctionType.Copy
+
+P = 128
+PACK = 4
+HALF = S // 2
+X_ROW = 4
+
+
+def tile_picked_dwlhopbpagq_none_p_kernel(tc, x_words, x_scales, d_words, d_scales, gn, w1, offs, ci, n1, n2, n3, n4, n5, out):
+    nc = tc.nc
+    with ExitStack() as ctx:
+        sb = ctx.enter_context(tc.tile_pool(name="sb", bufs=1))
+        ps = ctx.enter_context(tc.psum_pool(name="ps", bufs=1))
+
+        def load_list(name, src):
+            lst = sb.tile(list(src.shape), U16, name=name)
+            nc.sync.dma_start(lst[:], src)
+            return lst
+
+        def load_words(name, src):
+            tab = sb.tile([P, src.shape[2]], U32, name=name)
+            nc.sync.dma_start(tab[:].bitcast(I32), src[0].rearrange("p n r -> p (n r)").bitcast(I32))
+            return tab
+
+        def load_scales(name, src, row):
+            tab = sb.tile([P, src.shape[2]], U8, name=name)
+            nc.vector.memset(tab[:].bitcast(I32), 0)
+            for q in range(4):
+                nc.scalar.dma_start(tab[32 * q + row : 32 * q + row + 4, :].bitcast(I32), src[0, 4 * q : 4 * q + 4, :].bitcast(I32))
+            return tab
+
+        dw = load_words("dw", d_words)
+        ci_t = load_list("ci_t", ci)
+        xw = load_words("xw", x_words)
+        offs_t = load_list("offs_t", offs)
+        dsc = load_scales("dsc", d_scales, 0)
+        xsc = load_scales("xsc", x_scales, X_ROW)
+        n1_t = load_list("n1_t", n1)
+        gain = sb.tile([P, PACK], F32, name="gain")
+        nc.sync.dma_start(gain[:], gn.rearrange("(p t) o -> p (t o)", t=PACK))
+        n2_t = load_list("n2_t", n2)
+        w_raw = sb.tile([P, PACK, N], F32, name="w_raw")
+        nc.sync.dma_start(w_raw[:], w1.rearrange("(p t) m -> p t m", t=PACK))
+        n3_t = load_list("n3_t", n3)
+        n5_t = load_list("n5_t", n5)
+        n4_t = load_list("n4_t", n4)
+
+        d_sc = sb.tile([P, H], U8, name="d_sc", align_bytes=64)
+        x_sc = sb.tile([P, S], U8, name="x_sc", align_bytes=64)
+        d_q = sb.tile([P, H], U32, name="d_q", align_bytes=64)
+        x_q = sb.tile([P, S], U32, name="x_q", align_bytes=64)
+        nc.vector.tensor_copy(d_sc[:].rearrange("p (t m) -> p m t", t=PACK), dsc[:].indirect(ci_t[:]))
+        nc.vector.tensor_copy(d_q[:].rearrange("p (t m) -> p m t", t=PACK), dw[:].indirect(ci_t[:]))
+        nc.vector.tensor_copy(x_sc[:], xsc[:].indirect(offs_t[:]))
+        nc.vector.tensor_copy(x_q[:], xw[:].indirect(offs_t[:]))
+
+        half_gain = sb.tile([P, PACK], F32, name="half_gain")
+        nc.vector.tensor_scalar(half_gain[:], gain[:], -0.5, None, ALU.mult)
+
+        s_tiles, st_tiles = [], []
+        for t in range(PACK):
+            cols = slice(P * t, P * (t + 1))
+            acc = ps.tile([P, S], F32, name="s_acc%d" % t)
+            nc.tensor.matmul_mx(out=acc[:], lhsT=d_q[:, cols].bitcast(FP8X4), lhsT_scale=d_sc[:, cols],
+                                rhs=x_q[:].bitcast(FP8X4), rhs_scale=x_sc[X_ROW:P, :], start=True, stop=True)
+            s_t = sb.tile([P, 2 * S], F32, name="s%d" % t)
+            if t == 0:
+                nc.scalar.activation(s_t[:, 0:S], acc[:], COPY, scale=0.0625)
+            else:
+                nc.vector.tensor_scalar(s_t[:, 0:S], acc[:], 0.0625, None, ALU.mult)
+            s_tiles.append(s_t)
+        for t in range(PACK):
+            far = sb.tile([P, S], F32, name="far%d" % t)
+            nc.scalar.activation(far[:], s_tiles[t][:].indirect(n1_t[:]), COPY)
+            st_t = sb.tile([P, S], F32, name="st%d" % t)
+            nc.vector.tensor_tensor(st_t[:], s_tiles[t][:, 0:S], far[:], ALU.max)
+            st_tiles.append(st_t)
+
+        w_q = sb.tile([P, N], U32, name="w_q", align_bytes=64)
+        w_sc = sb.tile([P, N], U8, name="w_sc", align_bytes=64)
+
+        def quantise_w(mt):
+            cols = slice(P * mt, P * (mt + 1))
+            w_bf = sb.tile([P, P * PACK], BF16, name="w_bf%d" % mt, align_bytes=64)
+            nc.vector.tensor_copy(w_bf[:].rearrange("p (c i t) -> p c t i", i=4, t=PACK),
+                                  w_raw[:, :, cols].rearrange("p t (c i) -> p c t i", i=4))
+            nc.vector.quantize_mx(out=w_q[:, cols].bitcast(FP8X4), scales=w_sc[:, cols], in_=w_bf[:])
+
+        quantise_w(0)
+
+        z_q = sb.tile([P, S], U32, name="z_q", align_bytes=64)
+        z_sc = sb.tile([P, S], U8, name="z_sc", align_bytes=64)
+        h_acc = [ps.tile([P, S], F32, name="h_acc%d" % mt) for mt in range(N // P)]
+        h_tiles = [sb.tile([P, 2 * S], F32, name="h%d" % mt) for mt in range(N // P)]
+        pages = [sb.tile([P, U], F32, name="page%d" % mt) for mt in range(N // P)]
+
+        def layer(mt, cols):
+            rows = slice(P * mt, P * (mt + 1))
+            nc.tensor.matmul_mx(out=h_acc[mt][:, cols], lhsT=w_q[:, rows].bitcast(FP8X4), lhsT_scale=w_sc[:, rows],
+                                rhs=z_q[:, cols].bitcast(FP8X4), rhs_scale=z_sc[:, cols], start=True, stop=True)
+            nc.vector.tensor_copy(h_tiles[mt][:, cols], h_acc[mt][:, cols])
+
+        def put_h(mt, lo, hi):
+            nc.scalar.activation(pages[mt][:].indirect(n3_t[:, lo // 16 : hi // 16]), h_tiles[mt][:, lo:hi], COPY)
+
+        for u in range(2):
+            cols = slice(HALF * u, HALF * (u + 1))
+            z_rows = sb.tile([P, PACK, HALF], BF16, name="z_rows%d" % u)
+            for t in range(PACK):
+                hop = sb.tile([P, HALF], F32, name="hop%d_%d" % (u, t))
+                nc.scalar.activation(hop[:], st_tiles[t][:].indirect(n2_t[:, HALF * u // 16 : HALF * (u + 1) // 16]), COPY,
+                                     scale=gain[:, t : t + 1])
+                nc.vector.scalar_tensor_tensor(z_rows[:, t, :], s_tiles[t][:, cols], half_gain[:, t : t + 1], hop[:], ALU.mult, ALU.add)
+            z_bf = sb.tile([P, HALF * PACK], BF16, name="z_bf%d" % u, align_bytes=64)
+            nc.vector.tensor_copy(z_bf[:].rearrange("p (c i t) -> p c t i", i=4, t=PACK),
+                                  z_rows[:].rearrange("p t (c i) -> p c t i", i=4))
+            nc.vector.quantize_mx(out=z_q[:, cols].bitcast(FP8X4), scales=z_sc[:, cols], in_=z_bf[:])
+            layer(0, cols)
+        put_h(0, 0, HALF)
+
+        for mt in range(N // P):
+            if mt > 0:
+                quantise_w(mt)
+                layer(mt, slice(0, S))
+            other = sb.tile([P, S], F32, name="other%d" % mt)
+            nc.scalar.activation(other[:], h_tiles[mt][:].indirect(n5_t[:]), COPY)
+            nw = sb.tile([P, S], F32, name="nw%d" % mt)
+            nc.vector.tensor_tensor(nw[:], h_tiles[mt][:, 0:S], other[:], ALU.subtract)
+            put_h(mt, HALF if mt == 0 else 0, S)
+            nc.scalar.activation(pages[mt][:].indirect(n4_t[:]), nw[:], COPY)
+            nc.sync.dma_start(out[P * mt : P * (mt + 1), :], pages[mt][:])

@@ -19,6 +19,9 @@ P = 128
 PACK = 4
 HALF = S // 2
 X_ROW = 4
+W_STAGE = (1, 2, 1, 1)
+Z_STAGE = (0, 1)
+EARLY = 2
 
 
 def tile_picked_dwlhopbpagq_none_p_kernel(tc, x_words, x_scales, d_words, d_scales, gn, w1, offs, ci, n1, n2, n3, n4, n5, out):
@@ -37,37 +40,43 @@ def tile_picked_dwlhopbpagq_none_p_kernel(tc, x_words, x_scales, d_words, d_scal
             nc.sync.dma_start(tab[:].bitcast(I32), src[0].rearrange("p n r -> p (n r)").bitcast(I32))
             return tab
 
-        def load_scales(name, src, row):
-            tab = sb.tile([P, src.shape[2]], U8, name=name)
-            nc.vector.memset(tab[:].bitcast(I32), 0)
-            for q in range(4):
-                nc.scalar.dma_start(tab[32 * q + row : 32 * q + row + 4, :].bitcast(I32), src[0, 4 * q : 4 * q + 4, :].bitcast(I32))
-            return tab
-
-        dw = load_words("dw", d_words)
+        d_stage = sb.tile([P, 2, G], U8, name="d_stage")
+        for a in range(2):
+            nc.sync.dma_start(d_stage[64 * a : 64 * a + 4, :, :].bitcast(I32),
+                              d_scales[0, 8 * a : 8 * a + 8, :].rearrange("(q r) n -> r q n", q=2).bitcast(I32))
         ci_t = load_list("ci_t", ci)
-        xw = load_words("xw", x_words)
+        dw = load_words("dw", d_words)
+        xsc = sb.tile([P, T], U8, name="xsc", tag="x_bytes", align_bytes=64)
+        nc.vector.memset(xsc[:].bitcast(I32), 0)
+        for q in range(4):
+            nc.sync.dma_start(xsc[32 * q + X_ROW : 32 * q + X_ROW + 4, :].bitcast(I32), x_scales[0, 4 * q : 4 * q + 4, :].bitcast(I32))
         offs_t = load_list("offs_t", offs)
-        dsc = load_scales("dsc", d_scales, 0)
-        xsc = load_scales("xsc", x_scales, X_ROW)
+        xw = load_words("xw", x_words)
         n1_t = load_list("n1_t", n1)
+        w_raw = sb.tile([P, PACK, N], F32, name="w_raw")
+        nc.sync.dma_start(w_raw[:], w1.rearrange("(p t) m -> p t m", t=PACK))
         gain = sb.tile([P, PACK], F32, name="gain")
         nc.sync.dma_start(gain[:], gn.rearrange("(p t) o -> p (t o)", t=PACK))
         n2_t = load_list("n2_t", n2)
-        w_raw = sb.tile([P, PACK, N], F32, name="w_raw")
-        nc.sync.dma_start(w_raw[:], w1.rearrange("(p t) m -> p t m", t=PACK))
         n3_t = load_list("n3_t", n3)
         n5_t = load_list("n5_t", n5)
         n4_t = load_list("n4_t", n4)
 
+        dsc = sb.tile([P, G], U8, name="dsc", tag="d_bytes", align_bytes=64)
+        nc.vector.memset(dsc[:].bitcast(I32), 0)
+        for q in range(4):
+            src = 64 * (q // 2)
+            nc.vector.tensor_copy(dsc[32 * q : 32 * q + 4, :].bitcast(I32), d_stage[src : src + 4, q % 2, :].bitcast(I32))
+
         d_sc = sb.tile([P, H], U8, name="d_sc", align_bytes=64)
         x_sc = sb.tile([P, S], U8, name="x_sc", align_bytes=64)
-        d_q = sb.tile([P, H], U32, name="d_q", align_bytes=64)
-        x_q = sb.tile([P, S], U32, name="x_q", align_bytes=64)
+        d_q = sb.tile([P, H], U32, name="d_q", tag="d_bytes", align_bytes=64)
+        x_q = sb.tile([P, S], U32, name="x_q", tag="x_bytes", align_bytes=64)
         nc.vector.tensor_copy(d_sc[:].rearrange("p (t m) -> p m t", t=PACK), dsc[:].indirect(ci_t[:]))
         nc.vector.tensor_copy(d_q[:].rearrange("p (t m) -> p m t", t=PACK), dw[:].indirect(ci_t[:]))
         nc.vector.tensor_copy(x_sc[:], xsc[:].indirect(offs_t[:]))
-        nc.vector.tensor_copy(x_q[:], xw[:].indirect(offs_t[:]))
+        for u in range(2):
+            nc.vector.tensor_copy(x_q[:, HALF * u : HALF * (u + 1)], xw[:].indirect(offs_t[:, HALF * u // 16 : HALF * (u + 1) // 16]))
 
         half_gain = sb.tile([P, PACK], F32, name="half_gain")
         nc.vector.tensor_scalar(half_gain[:], gain[:], -0.5, None, ALU.mult)
@@ -75,17 +84,18 @@ def tile_picked_dwlhopbpagq_none_p_kernel(tc, x_words, x_scales, d_words, d_scal
         s_tiles, st_tiles = [], []
         for t in range(PACK):
             cols = slice(P * t, P * (t + 1))
-            acc = ps.tile([P, S], F32, name="s_acc%d" % t)
-            nc.tensor.matmul_mx(out=acc[:], lhsT=d_q[:, cols].bitcast(FP8X4), lhsT_scale=d_sc[:, cols],
-                                rhs=x_q[:].bitcast(FP8X4), rhs_scale=x_sc[X_ROW:P, :], start=True, stop=True)
             s_t = sb.tile([P, 2 * S], F32, name="s%d" % t)
-            if t == 0:
-                nc.scalar.activation(s_t[:, 0:S], acc[:], COPY, scale=0.0625)
-            else:
-                nc.vector.tensor_scalar(s_t[:, 0:S], acc[:], 0.0625, None, ALU.mult)
+            for lo, hi in ((0, HALF), (HALF, S)) if t == 0 else ((0, S),):
+                acc = ps.tile([P, hi - lo], F32, name="s_acc%d_%d" % (t, lo), tag="bank%d" % (t if lo == 0 else PACK))
+                nc.tensor.matmul_mx(out=acc[:], lhsT=d_q[:, cols].bitcast(FP8X4), lhsT_scale=d_sc[:, cols],
+                                    rhs=x_q[:, lo:hi].bitcast(FP8X4), rhs_scale=x_sc[X_ROW:P, lo:hi], start=True, stop=True)
+                if t == 0:
+                    nc.scalar.activation(s_t[:, lo:hi], acc[:], COPY, scale=0.0625)
+                else:
+                    nc.vector.tensor_scalar(s_t[:, lo:hi], acc[:], 0.0625, None, ALU.mult)
             s_tiles.append(s_t)
         for t in range(PACK):
-            far = sb.tile([P, S], F32, name="far%d" % t)
+            far = sb.tile([P, S], F32, name="far%d" % t, tag="stage%d" % t, align_bytes=64)
             nc.scalar.activation(far[:], s_tiles[t][:].indirect(n1_t[:]), COPY)
             st_t = sb.tile([P, S], F32, name="st%d" % t)
             nc.vector.tensor_tensor(st_t[:], s_tiles[t][:, 0:S], far[:], ALU.max)
@@ -96,24 +106,29 @@ def tile_picked_dwlhopbpagq_none_p_kernel(tc, x_words, x_scales, d_words, d_scal
 
         def quantise_w(mt):
             cols = slice(P * mt, P * (mt + 1))
-            w_bf = sb.tile([P, P * PACK], BF16, name="w_bf%d" % mt, align_bytes=64)
+            w_bf = sb.tile([P, P * PACK], BF16, name="w_bf%d" % mt, tag="stage%d" % W_STAGE[mt], align_bytes=64)
             nc.vector.tensor_copy(w_bf[:].rearrange("p (c i t) -> p c t i", i=4, t=PACK),
                                   w_raw[:, :, cols].rearrange("p t (c i) -> p c t i", i=4))
             nc.vector.quantize_mx(out=w_q[:, cols].bitcast(FP8X4), scales=w_sc[:, cols], in_=w_bf[:])
 
-        quantise_w(0)
+        for mt in range(EARLY):
+            quantise_w(mt)
 
         z_q = sb.tile([P, S], U32, name="z_q", align_bytes=64)
         z_sc = sb.tile([P, S], U8, name="z_sc", align_bytes=64)
-        h_acc = [ps.tile([P, S], F32, name="h_acc%d" % mt) for mt in range(N // P)]
-        h_tiles = [sb.tile([P, 2 * S], F32, name="h%d" % mt) for mt in range(N // P)]
+        h_acc = [ps.tile([P, S], F32, name="h_acc%d" % mt, tag="bank%d" % mt) for mt in range(N // P)]
+        h_pairs = [sb.tile([P, 2, 2 * S], F32, name="h%d" % a) for a in range(N // P // 2)]
+        h_tiles = [h_pairs[mt // 2][:, mt % 2, :] for mt in range(N // P)]
         pages = [sb.tile([P, U], F32, name="page%d" % mt) for mt in range(N // P)]
 
         def layer(mt, cols):
             rows = slice(P * mt, P * (mt + 1))
             nc.tensor.matmul_mx(out=h_acc[mt][:, cols], lhsT=w_q[:, rows].bitcast(FP8X4), lhsT_scale=w_sc[:, rows],
                                 rhs=z_q[:, cols].bitcast(FP8X4), rhs_scale=z_sc[:, cols], start=True, stop=True)
-            nc.vector.tensor_copy(h_tiles[mt][:, cols], h_acc[mt][:, cols])
+            if mt == 0 and cols.start == 0:
+                nc.scalar.copy(h_tiles[mt][:, cols], h_acc[mt][:, cols])
+            else:
+                nc.vector.tensor_copy(h_tiles[mt][:, cols], h_acc[mt][:, cols])
 
         def put_h(mt, lo, hi):
             nc.scalar.activation(pages[mt][:].indirect(n3_t[:, lo // 16 : hi // 16]), h_tiles[mt][:, lo:hi], COPY)
@@ -122,25 +137,29 @@ def tile_picked_dwlhopbpagq_none_p_kernel(tc, x_words, x_scales, d_words, d_scal
             cols = slice(HALF * u, HALF * (u + 1))
             z_rows = sb.tile([P, PACK, HALF], BF16, name="z_rows%d" % u)
             for t in range(PACK):
-                hop = sb.tile([P, HALF], F32, name="hop%d_%d" % (u, t))
+                hop = sb.tile([P, HALF], F32, name="hop%d_%d" % (u, t), tag="hop%d" % t)
                 nc.scalar.activation(hop[:], st_tiles[t][:].indirect(n2_t[:, HALF * u // 16 : HALF * (u + 1) // 16]), COPY,
                                      scale=gain[:, t : t + 1])
                 nc.vector.scalar_tensor_tensor(z_rows[:, t, :], s_tiles[t][:, cols], half_gain[:, t : t + 1], hop[:], ALU.mult, ALU.add)
-            z_bf = sb.tile([P, HALF * PACK], BF16, name="z_bf%d" % u, align_bytes=64)
+            z_bf = sb.tile([P, HALF * PACK], BF16, name="z_bf%d" % u, tag="stage%d" % Z_STAGE[u], align_bytes=64)
             nc.vector.tensor_copy(z_bf[:].rearrange("p (c i t) -> p c t i", i=4, t=PACK),
                                   z_rows[:].rearrange("p t (c i) -> p c t i", i=4))
             nc.vector.quantize_mx(out=z_q[:, cols].bitcast(FP8X4), scales=z_sc[:, cols], in_=z_bf[:])
-            layer(0, cols)
-        put_h(0, 0, HALF)
+            for mt in range(EARLY):
+                layer(mt, cols)
+                if u == 0:
+                    put_h(mt, 0, HALF)
 
-        for mt in range(N // P):
-            if mt > 0:
-                quantise_w(mt)
-                layer(mt, slice(0, S))
-            other = sb.tile([P, S], F32, name="other%d" % mt)
-            nc.scalar.activation(other[:], h_tiles[mt][:].indirect(n5_t[:]), COPY)
-            nw = sb.tile([P, S], F32, name="nw%d" % mt)
-            nc.vector.tensor_tensor(nw[:], h_tiles[mt][:, 0:S], other[:], ALU.subtract)
-            put_h(mt, HALF if mt == 0 else 0, S)
-            nc.scalar.activation(pages[mt][:].indirect(n4_t[:]), nw[:], COPY)
-            nc.sync.dma_start(out[P * mt : P * (mt + 1), :], pages[mt][:])
+        for a in range(N // P // 2):
+            other = sb.tile([P, 2, S], F32, name="other%d" % a)
+            nw = sb.tile([P, 2, S], F32, name="nw%d" % a)
+            for mt in (2 * a, 2 * a + 1):
+                if mt >= EARLY:
+                    quantise_w(mt)
+                    layer(mt, slice(0, S))
+                nc.scalar.activation(other[:, mt % 2, :], h_tiles[mt].indirect(n5_t[:]), COPY)
+                put_h(mt, HALF if mt < EARLY else 0, S)
+            nc.vector.tensor_tensor(nw[:], h_pairs[a][:, :, 0:S], other[:], ALU.subtract)
+            for mt in (2 * a, 2 * a + 1):
+                nc.scalar.activation(pages[mt][:].indirect(n4_t[:]), nw[:, mt % 2, :], COPY)
+                nc.sync.dma_start(out[P * mt : P * (mt + 1), :], pages[mt][:])

from contextlib import ExitStack

import concourse.mybir as mybir

K, T, G, S, H, N, U = 512, 2048, 2048, 256, 512, 512, 512
FLOPS = 2 * K * H * S + 2 * H * N * S

F32 = mybir.dt.float32
BF16 = mybir.dt.bfloat16
I32 = mybir.dt.int32
U32 = mybir.dt.uint32
U16 = mybir.dt.uint16
U8 = mybir.dt.uint8
FP8X4 = mybir.dt.float8_e4m3fn_x4
ALU = mybir.AluOpType
COPY = mybir.ActivationFunctionType.Copy

P = 128
PACK = 4
HALF = S // 2
X_ROW = 4
W_STAGE = (1, 2, 1, 1)
Z_STAGE = (0, 1)
EARLY = 2


def tile_picked_dwlhopbpagq_none_p_kernel(tc, x_words, x_scales, d_words, d_scales, gn, w1, offs, ci, n1, n2, n3, n4, n5, out):
    nc = tc.nc
    with ExitStack() as ctx:
        sb = ctx.enter_context(tc.tile_pool(name="sb", bufs=1))
        ps = ctx.enter_context(tc.psum_pool(name="ps", bufs=1))

        def load_list(name, src):
            lst = sb.tile(list(src.shape), U16, name=name)
            nc.sync.dma_start(lst[:], src)
            return lst

        def load_words(name, src):
            tab = sb.tile([P, src.shape[2]], U32, name=name)
            nc.sync.dma_start(tab[:].bitcast(I32), src[0].rearrange("p n r -> p (n r)").bitcast(I32))
            return tab

        d_stage = sb.tile([P, 2, G], U8, name="d_stage")
        for a in range(2):
            nc.sync.dma_start(d_stage[64 * a : 64 * a + 4, :, :].bitcast(I32),
                              d_scales[0, 8 * a : 8 * a + 8, :].rearrange("(q r) n -> r q n", q=2).bitcast(I32))
        ci_t = load_list("ci_t", ci)
        dw = load_words("dw", d_words)
        xsc = sb.tile([P, T], U8, name="xsc", tag="x_bytes", align_bytes=64)
        nc.vector.memset(xsc[:].bitcast(I32), 0)
        for q in range(4):
            nc.sync.dma_start(xsc[32 * q + X_ROW : 32 * q + X_ROW + 4, :].bitcast(I32), x_scales[0, 4 * q : 4 * q + 4, :].bitcast(I32))
        offs_t = load_list("offs_t", offs)
        xw = load_words("xw", x_words)
        n1_t = load_list("n1_t", n1)
        w_raw = sb.tile([P, PACK, N], F32, name="w_raw")
        nc.sync.dma_start(w_raw[:], w1.rearrange("(p t) m -> p t m", t=PACK))
        gain = sb.tile([P, PACK], F32, name="gain")
        nc.sync.dma_start(gain[:], gn.rearrange("(p t) o -> p (t o)", t=PACK))
        n2_t = load_list("n2_t", n2)
        n3_t = load_list("n3_t", n3)
        n5_t = load_list("n5_t", n5)
        n4_t = load_list("n4_t", n4)

        dsc = sb.tile([P, G], U8, name="dsc", tag="d_bytes", align_bytes=64)
        nc.vector.memset(dsc[:].bitcast(I32), 0)
        for q in range(4):
            src = 64 * (q // 2)
            nc.vector.tensor_copy(dsc[32 * q : 32 * q + 4, :].bitcast(I32), d_stage[src : src + 4, q % 2, :].bitcast(I32))

        d_sc = sb.tile([P, H], U8, name="d_sc", align_bytes=64)
        x_sc = sb.tile([P, S], U8, name="x_sc", align_bytes=64)
        d_q = sb.tile([P, H], U32, name="d_q", tag="d_bytes", align_bytes=64)
        x_q = sb.tile([P, S], U32, name="x_q", tag="x_bytes", align_bytes=64)
        nc.vector.tensor_copy(d_sc[:].rearrange("p (t m) -> p m t", t=PACK), dsc[:].indirect(ci_t[:]))
        nc.vector.tensor_copy(d_q[:].rearrange("p (t m) -> p m t", t=PACK), dw[:].indirect(ci_t[:]))
        nc.vector.tensor_copy(x_sc[:], xsc[:].indirect(offs_t[:]))
        for u in range(2):
            nc.vector.tensor_copy(x_q[:, HALF * u : HALF * (u + 1)], xw[:].indirect(offs_t[:, HALF * u // 16 : HALF * (u + 1) // 16]))

        half_gain = sb.tile([P, PACK], F32, name="half_gain")
        nc.vector.tensor_scalar(half_gain[:], gain[:], -0.5, None, ALU.mult)

        s_tiles, st_tiles = [], []
        for t in range(PACK):
            cols = slice(P * t, P * (t + 1))
            s_t = sb.tile([P, 2 * S], F32, name="s%d" % t)
            for lo, hi in ((0, HALF), (HALF, S)) if t == 0 else ((0, S),):
                acc = ps.tile([P, hi - lo], F32, name="s_acc%d_%d" % (t, lo), tag="bank%d" % (t if lo == 0 else PACK))
                nc.tensor.matmul_mx(out=acc[:], lhsT=d_q[:, cols].bitcast(FP8X4), lhsT_scale=d_sc[:, cols],
                                    rhs=x_q[:, lo:hi].bitcast(FP8X4), rhs_scale=x_sc[X_ROW:P, lo:hi], start=True, stop=True)
                if t == 0:
                    nc.scalar.activation(s_t[:, lo:hi], acc[:], COPY, scale=0.0625)
                else:
                    nc.vector.tensor_scalar(s_t[:, lo:hi], acc[:], 0.0625, None, ALU.mult)
            s_tiles.append(s_t)
        for t in range(PACK):
            far = sb.tile([P, S], F32, name="far%d" % t, tag="stage%d" % t, align_bytes=64)
            nc.scalar.activation(far[:], s_tiles[t][:].indirect(n1_t[:]), COPY)
            st_t = sb.tile([P, S], F32, name="st%d" % t)
            nc.vector.tensor_tensor(st_t[:], s_tiles[t][:, 0:S], far[:], ALU.max)
            st_tiles.append(st_t)

        w_q = sb.tile([P, N], U32, name="w_q", align_bytes=64)
        w_sc = sb.tile([P, N], U8, name="w_sc", align_bytes=64)

        def quantise_w(mt):
            cols = slice(P * mt, P * (mt + 1))
            w_bf = sb.tile([P, P * PACK], BF16, name="w_bf%d" % mt, tag="stage%d" % W_STAGE[mt], align_bytes=64)
            nc.vector.tensor_copy(w_bf[:].rearrange("p (c i t) -> p c t i", i=4, t=PACK),
                                  w_raw[:, :, cols].rearrange("p t (c i) -> p c t i", i=4))
            nc.vector.quantize_mx(out=w_q[:, cols].bitcast(FP8X4), scales=w_sc[:, cols], in_=w_bf[:])

        for mt in range(EARLY):
            quantise_w(mt)

        z_q = sb.tile([P, S], U32, name="z_q", align_bytes=64)
        z_sc = sb.tile([P, S], U8, name="z_sc", align_bytes=64)
        h_acc = [ps.tile([P, S], F32, name="h_acc%d" % mt, tag="bank%d" % mt) for mt in range(N // P)]
        h_pairs = [sb.tile([P, 2, 2 * S], F32, name="h%d" % a) for a in range(N // P // 2)]
        h_tiles = [h_pairs[mt // 2][:, mt % 2, :] for mt in range(N // P)]
        pages = [sb.tile([P, U], F32, name="page%d" % mt) for mt in range(N // P)]

        def layer(mt, cols):
            rows = slice(P * mt, P * (mt + 1))
            nc.tensor.matmul_mx(out=h_acc[mt][:, cols], lhsT=w_q[:, rows].bitcast(FP8X4), lhsT_scale=w_sc[:, rows],
                                rhs=z_q[:, cols].bitcast(FP8X4), rhs_scale=z_sc[:, cols], start=True, stop=True)
            if mt == 0 and cols.start == 0:
                nc.scalar.copy(h_tiles[mt][:, cols], h_acc[mt][:, cols])
            else:
                nc.vector.tensor_copy(h_tiles[mt][:, cols], h_acc[mt][:, cols])

        def put_h(mt, lo, hi):
            nc.scalar.activation(pages[mt][:].indirect(n3_t[:, lo // 16 : hi // 16]), h_tiles[mt][:, lo:hi], COPY)

        for u in range(2):
            cols = slice(HALF * u, HALF * (u + 1))
            z_rows = sb.tile([P, PACK, HALF], BF16, name="z_rows%d" % u)
            for t in range(PACK):
                hop = sb.tile([P, HALF], F32, name="hop%d_%d" % (u, t), tag="hop%d" % t)
                nc.scalar.activation(hop[:], st_tiles[t][:].indirect(n2_t[:, HALF * u // 16 : HALF * (u + 1) // 16]), COPY,
                                     scale=gain[:, t : t + 1])
                nc.vector.scalar_tensor_tensor(z_rows[:, t, :], s_tiles[t][:, cols], half_gain[:, t : t + 1], hop[:], ALU.mult, ALU.add)
            z_bf = sb.tile([P, HALF * PACK], BF16, name="z_bf%d" % u, tag="stage%d" % Z_STAGE[u], align_bytes=64)
            nc.vector.tensor_copy(z_bf[:].rearrange("p (c i t) -> p c t i", i=4, t=PACK),
                                  z_rows[:].rearrange("p t (c i) -> p c t i", i=4))
            nc.vector.quantize_mx(out=z_q[:, cols].bitcast(FP8X4), scales=z_sc[:, cols], in_=z_bf[:])
            for mt in range(EARLY):
                layer(mt, cols)
                if u == 0:
                    put_h(mt, 0, HALF)

        for a in range(N // P // 2):
            other = sb.tile([P, 2, S], F32, name="other%d" % a)
            nw = sb.tile([P, 2, S], F32, name="nw%d" % a)
            for mt in (2 * a, 2 * a + 1):
                if mt >= EARLY:
                    quantise_w(mt)
                    layer(mt, slice(0, S))
                nc.scalar.activation(other[:, mt % 2, :], h_tiles[mt].indirect(n5_t[:]), COPY)
                put_h(mt, HALF if mt < EARLY else 0, S)
            nc.vector.tensor_tensor(nw[:], h_pairs[a][:, :, 0:S], other[:], ALU.subtract)
            for mt in (2 * a, 2 * a + 1):
                nc.scalar.activation(pages[mt][:].indirect(n4_t[:]), nw[:, mt % 2, :], COPY)
                nc.sync.dma_start(out[P * mt : P * (mt + 1), :], pages[mt][:])
